import numpy as np
import ml_dtypes


def mxq(x, axis, fmt="e4m3"):
    dtype, down = {"e4m3": (ml_dtypes.float8_e4m3fn, 7), "e5m2": (ml_dtypes.float8_e5m2, 14)}[fmt]
    v = np.moveaxis(np.asarray(x, np.float32).astype(ml_dtypes.bfloat16).astype(np.float64), axis, -1)
    blocks = v.reshape(v.shape[:-1] + (-1, 32))
    amax = np.abs(blocks).max(-1, keepdims=True)
    byte = np.maximum(np.where(amax > 0, np.frexp(amax)[1] - 1 + 127, 0) - down, 1)
    scale = np.exp2(byte - 127.0)
    codes = (blocks / scale).astype(np.float32).astype(dtype).astype(np.float64)
    return np.moveaxis((codes * scale).reshape(v.shape), -1, axis)


WIDE = False


def mx_kscale(k):
    if not WIDE:
        return np.ones(k)
    levels = np.array([10, -10, 5, -5, 0])
    if k % 512:
        return np.exp2(np.random.permutation(np.resize(levels, k // 32))).repeat(32)
    a = np.empty((k // 512, 16))
    for p in range(k // 512):
        a[p, :8] = np.random.permutation(np.resize(levels, 8))
        for g in range(8):
            far = levels[np.abs(levels - a[p, g]) >= 10]
            a[p, g + 8] = far[np.random.randint(len(far))]
    return np.exp2(a.ravel()).repeat(32)


def f64(x):
    return np.asarray(x).astype(np.float64)


def striped8(idx):
    return np.concatenate([x.reshape(-1, 16).T for x in idx]).astype(np.uint16)


def runs(offs, k):
    lists = np.stack([offs[16 * r : 16 * r + 16].T.reshape(-1) for r in range(8)]).astype(np.int64)
    return lists[np.arange(k) % 512 // 64]


def pack_weight(w):
    k, n = w.shape
    w = f64(np.asarray(w, np.float32).astype(ml_dtypes.bfloat16)).reshape(k // 32, 32, n)
    amax = np.abs(w).max(1)
    byte = np.clip(np.where(amax > 0, np.frexp(amax)[1] - 1 + 127 - 7, 1), 1, 254)
    scaled = (w * np.exp2(127.0 - byte)[:, None, :]).reshape(k, n).astype(np.float32)
    words = np.ascontiguousarray(scaled.reshape(k // 512, 128, 4, n).transpose(0, 1, 3, 2)).astype(ml_dtypes.float8_e4m3fn).view(np.uint8)
    return words, np.ascontiguousarray(byte.astype(np.uint8).reshape(k // 512, 16, n))


def unpack_weight(words, scales):
    g, p, n, _ = words.shape
    vals = np.ascontiguousarray(words).view(ml_dtypes.float8_e4m3fn).astype(np.float64) * np.repeat(np.exp2(scales.astype(np.float64) - 127.0), 8, axis=1)[..., None]
    return vals.transpose(0, 1, 3, 2).reshape(g * 512, n)

def planes(y):
    n, m = y.shape
    v = y.astype(np.float32).astype(ml_dtypes.bfloat16).astype(np.float64).reshape(n // 32, 32, m)
    top = np.abs(v).max(1)
    byte = np.clip(np.where(top > 0, np.frexp(top)[1] - 1 + 127 - 7, 1), 1, 254)
    codes = (v * np.exp2(127.0 - byte)[:, None, :]).reshape(n, m).astype(np.float32).astype(ml_dtypes.float8_e4m3fn).view(np.uint8)
    words = codes.reshape(n // 512, 128, 4, m).transpose(0, 1, 3, 2)
    return np.ascontiguousarray(words), np.ascontiguousarray(byte.astype(np.uint8).reshape(n // 512, 16, m))


K, T, S, N, W = 512, 2048, 512, 512, 256


def setup_inputs():
    n = np.random.standard_normal
    s = mx_kscale(K)[:, None]
    packed_xT = pack_weight(n((K, T)) * s)
    perm = np.stack([np.random.permutation(S) for _ in range(8)])
    return {
        "x_words": packed_xT[0],
        "x_scales": packed_xT[1],
        "w1": (n((K, N)) / np.sqrt(2 * K) / s).astype(np.float32),
        "w2": (n((K, N)) / np.sqrt(2 * K) / s).astype(np.float32),
        "offs": striped8(np.random.randint(0, T, (8, S))),
        "hz": striped8(np.random.randint(0, T, (8, S))),
        "n1": striped8(perm[:, :W]),
        "n2": striped8(perm[:, W:]),
    }


def reference(x_words, x_scales, w1, w2, offs, hz, n1, n2):
    xq = unpack_weight(x_words, x_scales)[np.arange(K)[:, None], runs(offs, K)]
    x_hz = unpack_weight(x_words, x_scales)[np.arange(K)[:, None], runs(hz, K)]
    h = mxq(f64(w1), 0, "e4m3").T @ xq + mxq(f64(w2), 0, "e4m3").T @ x_hz
    pa = h[np.arange(N)[:, None], runs(n1, N)]
    pb = h[np.arange(N)[:, None], runs(n2, N)]
    rb = np.maximum(pa, pb)
    ra = pa / (np.abs(pb) + 0.5)
    ds = np.zeros((N, S))
    ds[np.arange(N)[:, None], runs(n1, N)] = ra
    out = ds.copy()
    out[np.arange(N)[:, None], runs(n2, N)] = rb
    return (out,) + planes(out)

@@ -1,0 +1,164 @@
+from contextlib import ExitStack
+
+import concourse.mybir as mybir
+
+K, T, S, N, W = 512, 2048, 512, 512, 256
+FLOPS = 2 * 2 * K * N * S
+
+F32 = mybir.dt.float32
+BF16 = mybir.dt.bfloat16
+I32 = mybir.dt.int32
+U32 = mybir.dt.uint32
+U16 = mybir.dt.uint16
+U8 = mybir.dt.uint8
+FP8X4 = mybir.dt.float8_e4m3fn_x4
+ACT = mybir.ActivationFunctionType
+ALU = mybir.AluOpType
+
+P = 128
+PACK = 4
+M_VECTOR = 88
+
+
+def tile_picked_ohhratio_none_po_kernel(
+    tc, x_words, x_scales, w1, w2, offs, hz, n1, n2, out_0, out_1, out_2
+):
+    nc = tc.nc
+    with ExitStack() as ctx:
+        keep = ctx.enter_context(tc.tile_pool(name="keep", bufs=1))
+        psum = ctx.enter_context(tc.psum_pool(name="psum", bufs=1))
+
+        offs_sb = keep.tile([P, S // 16], U16, name="offs_sb")
+        hz_sb = keep.tile([P, S // 16], U16, name="hz_sb")
+        n1_sb = keep.tile([P, W // 16], U16, name="n1_sb")
+        n2_sb = keep.tile([P, W // 16], U16, name="n2_sb")
+        scale_table = keep.tile([P, T], U8, name="scale_table", align_bytes=64)
+        word_table = keep.tile([P, T], U32, name="word_table", align_bytes=64)
+        x_plane = keep.tile([P, 2 * S], U8, name="x_plane", align_bytes=64)
+        raw = [keep.tile([P, PACK, N], F32, name=f"raw{i}", align_bytes=64) for i in range(2)]
+
+        nc.gpsimd.memset(scale_table[:].bitcast(I32), 0)
+        nc.gpsimd.memset(x_plane[:].bitcast(I32), 0)
+        nc.sync.dma_start(offs_sb[:], offs)
+        nc.sync.dma_start(hz_sb[:], hz)
+        nc.scalar.dma_start(scale_table[0:P:8, :].bitcast(I32), x_scales[0].bitcast(I32))
+        nc.sync.dma_start(word_table[:].bitcast(I32), x_words[0].rearrange("p c r -> p (c r)").bitcast(I32))
+        nc.sync.dma_start(n1_sb[:], n1)
+        nc.sync.dma_start(n2_sb[:], n2)
+        for i, w in enumerate((w1, w2)):
+            nc.sync.dma_start(raw[i][:], w.rearrange("(p j) m -> p j m", j=PACK))
+
+        picked_scales = keep.tile([P, 2 * S], U8, name="picked_scales", align_bytes=64)
+        picked_words = [keep.tile([P, S], U32, name=f"picked_words{i}", align_bytes=64) for i in range(2)]
+        lists = (offs_sb, hz_sb)
+        for i in range(2):
+            nc.vector.tensor_copy(picked_scales[:, i * S : (i + 1) * S], scale_table[:].indirect(lists[i][:]))
+        for i in range(PACK):
+            nc.scalar.dma_start(x_plane[i:P:32, :].bitcast(I32), picked_scales[8 * i : P : 32, :].bitcast(I32))
+        for i in range(2):
+            nc.vector.tensor_copy(picked_words[i][:], word_table[:].indirect(lists[i][:]))
+
+        first = [psum.tile([P, W], F32, name=f"first{c}") for c in range(2)]
+        banks = [None] + [psum.tile([P, S], F32, name=f"bank{t}") for t in range(1, PACK)]
+        vector_share = {(0, 0): P, (0, 1): 0, (1, 0): M_VECTOR, (1, 1): P}
+        for half in range(2):
+            for i in range(2):
+                grouped = keep.tile([P, 2, P, PACK], BF16, name=f"grouped{i}{half}", align_bytes=64)
+                codes = keep.tile([P, 2 * P], U32, name=f"codes{i}{half}", align_bytes=64)
+                scales = keep.tile([P, 2 * P], U8, name=f"scales{i}{half}", align_bytes=64)
+                src = raw[i][:].rearrange("p j (m t) -> p m j t", t=PACK)[:, :, :, 2 * half : 2 * half + 2]
+                dst = grouped[:].rearrange("p t m j -> p m j t")
+                share = vector_share[(i, half)]
+                if share > 0:
+                    nc.vector.tensor_copy(dst[:, :share], src[:, :share])
+                if share < P:
+                    nc.scalar.copy(dst[:, share:], src[:, share:])
+                nc.vector.quantize_mx(codes[:].bitcast(FP8X4), scales[:], grouped[:].rearrange("p t m j -> p (t m j)"))
+                for u in range(2):
+                    t = 2 * half + u
+                    parts = [(first[c], c * W, W) for c in range(2)] if t == 0 else [(banks[t], 0, S)]
+                    for bank, c0, width in parts:
+                        nc.tensor.matmul_mx(
+                            out=bank[:],
+                            lhsT=codes[:, u * P : (u + 1) * P].bitcast(FP8X4),
+                            lhsT_scale=scales[:, u * P : (u + 1) * P],
+                            rhs=picked_words[i][:, c0 : c0 + width].bitcast(FP8X4),
+                            rhs_scale=x_plane[:, i * S + c0 : i * S + c0 + width],
+                            start=(i == 0),
+                            stop=(i == 1),
+                        )
+
+        h = [keep.tile([P, S], F32, name=f"h{t}") for t in range(PACK)]
+        pa = [keep.tile([P, W], F32, name=f"pa{t}") for t in range(PACK)]
+        pb = [keep.tile([P, W], F32, name=f"pb{t}") for t in range(PACK)]
+        size = [keep.tile([P, W], F32, name=f"size{t}") for t in range(PACK)]
+        root = [keep.tile([P, W], F32, name=f"root{t}") for t in range(PACK)]
+        inv = [keep.tile([P, W], F32, name=f"inv{t}") for t in range(PACK)]
+        larger = [keep.tile([P, W], F32, name=f"larger{t}") for t in range(PACK)]
+        y = [keep.tile([P, S], F32, name=f"y{t}") for t in range(PACK)]
+        rows = out_0.rearrange("(p t) c -> p t c", t=PACK)
+
+        def fetch_steps(t):
+            return [
+                lambda: nc.scalar.copy(h[t][:], banks[t][:]),
+                lambda: nc.scalar.activation(pb[t][:], h[t][:].indirect(n2_sb[:]), ACT.Copy),
+                lambda: nc.scalar.activation(pa[t][:], h[t][:].indirect(n1_sb[:]), ACT.Copy),
+            ]
+
+        def inverse_steps(t):
+            return [
+                lambda: nc.scalar.activation(size[t][:], pb[t][:], ACT.Abs),
+                lambda: nc.scalar.activation(root[t][:], size[t][:], ACT.Abs_reciprocal_sqrt, bias=0.5),
+                lambda: nc.scalar.activation(inv[t][:], root[t][:], ACT.Square),
+            ]
+
+        nc.vector.tensor_copy(h[0][:, :W], first[0][:])
+        nc.scalar.copy(h[0][:, W:], first[1][:])
+        nc.scalar.activation(pb[0][:], h[0][:].indirect(n2_sb[:]), ACT.Copy)
+        nc.vector.tensor_copy(pa[0][:], h[0][:].indirect(n1_sb[:]))
+        for t in range(PACK):
+            if t + 1 < PACK:
+                for fetch, inverse in zip(fetch_steps(t + 1), inverse_steps(t)):
+                    fetch()
+                    inverse()
+            else:
+                for inverse in inverse_steps(t):
+                    inverse()
+
+        def put_larger(t):
+            nc.vector.tensor_copy(y[t][:].indirect(n2_sb[:]), larger[t][:])
+
+        def put_ratio(t):
+            nc.vector.tensor_tensor(y[t][:].indirect(n1_sb[:]), pa[t][:], inv[t][:], ALU.mult)
+            nc.sync.dma_start(rows[:, t, :], y[t][:])
+
+        for t in range(PACK):
+            nc.vector.tensor_tensor(larger[t][:], pa[t][:], pb[t][:], ALU.max)
+            if t > 0:
+                put_ratio(t - 1)
+            put_larger(t)
+        put_ratio(PACK - 1)
+
+        pairs = keep.tile([P, 2, S, 2], BF16, name="pairs", align_bytes=64)
+        y_grouped = keep.tile([P, S, 2], I32, name="y_grouped", align_bytes=64)
+        y_codes = keep.tile([P, S], U32, name="y_codes", align_bytes=64)
+        y_scales = keep.tile([P, S], U8, name="y_scales", align_bytes=64)
+        word_rows = out_1[0].rearrange("p c r -> p (c r)").bitcast(I32)
+        pair_words = pairs[:].rearrange("p u c e -> p u (c e)").bitcast(I32)
+        for t in range(PACK - 1):
+            nc.scalar.copy(pairs[:, t // 2, :, t % 2], y[t][:])
+        halves = [slice(c * W, (c + 1) * W) for c in range(2)]
+        for cols in halves:
+            nc.scalar.copy(pairs[:, 1, cols, 1], y[PACK - 1][:, cols])
+        for cols in halves:
+            nc.vector.tensor_copy(y_grouped[:, cols, :], pair_words[:, :, cols].rearrange("p u c -> p c u"))
+        for cols in halves:
+            nc.vector.quantize_mx(
+                y_codes[:, cols].bitcast(FP8X4),
+                y_scales[:, cols],
+                y_grouped[:, cols, :].rearrange("p c u -> p (c u)").bitcast(BF16),
+            )
+            nc.sync.dma_start(word_rows[:, cols], y_codes[:, cols].bitcast(I32))
+        for q in range(4):
+            queue = nc.sync if q % 2 == 0 else nc.scalar
+            queue.dma_start(out_2[0][4 * q : 4 * q + 4, :].bitcast(I32), y_scales[32 * q : 32 * q + 4, :].bitcast(I32))

@@ -17,7 +17,6 @@ ALU = mybir.AluOpType
 
 P = 128
 PACK = 4
-M_VECTOR = 88
 
 
 def tile_picked_ohhratio_none_po_kernel(
@@ -37,16 +36,16 @@ def tile_picked_ohhratio_none_po_kernel(
         x_plane = keep.tile([P, 2 * S], U8, name="x_plane", align_bytes=64)
         raw = [keep.tile([P, PACK, N], F32, name=f"raw{i}", align_bytes=64) for i in range(2)]
 
-        nc.gpsimd.memset(scale_table[:].bitcast(I32), 0)
-        nc.gpsimd.memset(x_plane[:].bitcast(I32), 0)
+        nc.vector.memset(scale_table[:].bitcast(I32), 0)
+        nc.vector.memset(x_plane[:].bitcast(I32), 0)
         nc.sync.dma_start(offs_sb[:], offs)
         nc.sync.dma_start(hz_sb[:], hz)
         nc.scalar.dma_start(scale_table[0:P:8, :].bitcast(I32), x_scales[0].bitcast(I32))
         nc.sync.dma_start(word_table[:].bitcast(I32), x_words[0].rearrange("p c r -> p (c r)").bitcast(I32))
-        nc.sync.dma_start(n1_sb[:], n1)
-        nc.sync.dma_start(n2_sb[:], n2)
         for i, w in enumerate((w1, w2)):
             nc.sync.dma_start(raw[i][:], w.rearrange("(p j) m -> p j m", j=PACK))
+        nc.sync.dma_start(n2_sb[:], n2)
+        nc.sync.dma_start(n1_sb[:], n1)
 
         picked_scales = keep.tile([P, 2 * S], U8, name="picked_scales", align_bytes=64)
         picked_words = [keep.tile([P, S], U32, name=f"picked_words{i}", align_bytes=64) for i in range(2)]
@@ -58,35 +57,53 @@ def tile_picked_ohhratio_none_po_kernel(
         for i in range(2):
             nc.vector.tensor_copy(picked_words[i][:], word_table[:].indirect(lists[i][:]))
 
+        grouped = [[keep.tile([P, 2, P, PACK], BF16, name=f"grouped{i}{half}", align_bytes=64) for half in range(2)] for i in range(2)]
+        codes = [[keep.tile([P, 2 * P], U32, name=f"codes{i}{half}", align_bytes=64) for half in range(2)] for i in range(2)]
+        scales = [[keep.tile([P, 2 * P], U8, name=f"scales{i}{half}", align_bytes=64) for half in range(2)] for i in range(2)]
+
+        def deal(i, half, on_vector):
+            src = raw[i][:].rearrange("p j (m t) -> p m j t", t=PACK)[:, :, :, 2 * half : 2 * half + 2]
+            dst = grouped[i][half][:].rearrange("p t m j -> p m j t")
+            if on_vector > 0:
+                nc.vector.tensor_copy(dst[:, :on_vector], src[:, :on_vector])
+            nc.scalar.copy(dst[:, on_vector:], src[:, on_vector:])
+
+        def quantise(i, half, u0=0, u1=2):
+            nc.vector.quantize_mx(
+                codes[i][half][:, u0 * P : u1 * P].bitcast(FP8X4),
+                scales[i][half][:, u0 * P : u1 * P],
+                grouped[i][half][:, u0:u1].rearrange("p t m j -> p (t m j)"),
+            )
+
+        def product(bank, t, c0, width, order):
+            half, cols = t // 2, slice(t % 2 * P, (t % 2 + 1) * P)
+            for i in order:
+                nc.tensor.matmul_mx(
+                    out=bank[:],
+                    lhsT=codes[i][half][:, cols].bitcast(FP8X4),
+                    lhsT_scale=scales[i][half][:, cols],
+                    rhs=picked_words[i][:, c0 : c0 + width].bitcast(FP8X4),
+                    rhs_scale=x_plane[:, i * S + c0 : i * S + c0 + width],
+                    start=(i == order[0]),
+                    stop=(i == order[1]),
+                )
+
+        deal(0, 0, 0)
+        deal(0, 1, 64)
+        quantise(0, 0)
+        deal(1, 0, 88)
+        quantise(1, 0, 0, 1)
+        quantise(1, 0, 1, 2)
+        quantise(0, 1)
+        deal(1, 1, 32)
+        quantise(1, 1)
+
         first = [psum.tile([P, W], F32, name=f"first{c}") for c in range(2)]
-        banks = [None] + [psum.tile([P, S], F32, name=f"bank{t}") for t in range(1, PACK)]
-        vector_share = {(0, 0): P, (0, 1): 0, (1, 0): M_VECTOR, (1, 1): P}
-        for half in range(2):
-            for i in range(2):
-                grouped = keep.tile([P, 2, P, PACK], BF16, name=f"grouped{i}{half}", align_bytes=64)
-                codes = keep.tile([P, 2 * P], U32, name=f"codes{i}{half}", align_bytes=64)
-                scales = keep.tile([P, 2 * P], U8, name=f"scales{i}{half}", align_bytes=64)
-                src = raw[i][:].rearrange("p j (m t) -> p m j t", t=PACK)[:, :, :, 2 * half : 2 * half + 2]
-                dst = grouped[:].rearrange("p t m j -> p m j t")
-                share = vector_share[(i, half)]
-                if share > 0:
-                    nc.vector.tensor_copy(dst[:, :share], src[:, :share])
-                if share < P:
-                    nc.scalar.copy(dst[:, share:], src[:, share:])
-                nc.vector.quantize_mx(codes[:].bitcast(FP8X4), scales[:], grouped[:].rearrange("p t m j -> p (t m j)"))
-                for u in range(2):
-                    t = 2 * half + u
-                    parts = [(first[c], c * W, W) for c in range(2)] if t == 0 else [(banks[t], 0, S)]
-                    for bank, c0, width in parts:
-                        nc.tensor.matmul_mx(
-                            out=bank[:],
-                            lhsT=codes[:, u * P : (u + 1) * P].bitcast(FP8X4),
-                            lhsT_scale=scales[:, u * P : (u + 1) * P],
-                            rhs=picked_words[i][:, c0 : c0 + width].bitcast(FP8X4),
-                            rhs_scale=x_plane[:, i * S + c0 : i * S + c0 + width],
-                            start=(i == 0),
-                            stop=(i == 1),
-                        )
+        banks = {t: psum.tile([P, S], F32, name=f"bank{t}") for t in range(1, PACK)}
+        for c in range(2):
+            product(first[c], 0, c * W, W, (0, 1))
+        for t in range(1, PACK):
+            product(banks[t], t, 0, S, (1, 0))
 
         h = [keep.tile([P, S], F32, name=f"h{t}") for t in range(PACK)]
         pa = [keep.tile([P, W], F32, name=f"pa{t}") for t in range(PACK)]
@@ -160,5 +177,5 @@ def tile_picked_ohhratio_none_po_kernel(
             )
             nc.sync.dma_start(word_rows[:, cols], y_codes[:, cols].bitcast(I32))
         for q in range(4):
-            queue = nc.sync if q % 2 == 0 else nc.scalar
+            queue = nc.sync if q == 0 else nc.scalar
             queue.dma_start(out_2[0][4 * q : 4 * q + 4, :].bitcast(I32), y_scales[32 * q : 32 * q + 4, :].bitcast(I32))

@@ -37,15 +37,20 @@ def tile_picked_ohhratio_none_po_kernel(
         raw = [keep.tile([P, PACK, N], F32, name=f"raw{i}", align_bytes=64) for i in range(2)]
 
         nc.vector.memset(scale_table[:].bitcast(I32), 0)
-        nc.vector.memset(x_plane[:].bitcast(I32), 0)
+        nc.gpsimd.memset(x_plane[:].bitcast(I32), 0)
+        w1_rows = w1.rearrange("(p j) m -> p j m", j=PACK)
+        nc.sync.dma_start(raw[0][:, 0:2, :], w1_rows[:, 0:2, :])
         nc.sync.dma_start(offs_sb[:], offs)
         nc.sync.dma_start(hz_sb[:], hz)
-        nc.scalar.dma_start(scale_table[0:P:8, :].bitcast(I32), x_scales[0].bitcast(I32))
+        nc.sync.dma_start(scale_table[0:P:8, :].bitcast(I32), x_scales[0].bitcast(I32))
+        warm_in = keep.tile([P, 1], F32, name="warm_in")
+        warm_out = keep.tile([P, 1], F32, name="warm_out")
+        nc.gpsimd.memset(warm_in[:], 1.0)
+        nc.scalar.activation(warm_out[:], warm_in[:], ACT.Abs_reciprocal_sqrt, bias=0.5)
         nc.sync.dma_start(word_table[:].bitcast(I32), x_words[0].rearrange("p c r -> p (c r)").bitcast(I32))
-        for i, w in enumerate((w1, w2)):
-            nc.sync.dma_start(raw[i][:], w.rearrange("(p j) m -> p j m", j=PACK))
-        nc.sync.dma_start(n2_sb[:], n2)
-        nc.sync.dma_start(n1_sb[:], n1)
+        w2_rows = w2.rearrange("(p j) m -> p j m", j=PACK)
+        nc.sync.dma_start(raw[0][:, 2:4, :], w1_rows[:, 2:4, :])
+        nc.sync.dma_start(raw[1][:, 0:3, :], w2_rows[:, 0:3, :])
 
         picked_scales = keep.tile([P, 2 * S], U8, name="picked_scales", align_bytes=64)
         picked_words = [keep.tile([P, S], U32, name=f"picked_words{i}", align_bytes=64) for i in range(2)]
@@ -53,7 +58,11 @@ def tile_picked_ohhratio_none_po_kernel(
         for i in range(2):
             nc.vector.tensor_copy(picked_scales[:, i * S : (i + 1) * S], scale_table[:].indirect(lists[i][:]))
         for i in range(PACK):
-            nc.scalar.dma_start(x_plane[i:P:32, :].bitcast(I32), picked_scales[8 * i : P : 32, :].bitcast(I32))
+            queue = nc.sync if i % 2 == 0 else nc.scalar
+            queue.dma_start(x_plane[i:P:32, :].bitcast(I32), picked_scales[8 * i : P : 32, :].bitcast(I32))
+        nc.sync.dma_start(raw[1][:, 3:4, :], w2_rows[:, 3:4, :])
+        nc.sync.dma_start(n2_sb[:], n2)
+        nc.sync.dma_start(n1_sb[:], n1)
         for i in range(2):
             nc.vector.tensor_copy(picked_words[i][:], word_table[:].indirect(lists[i][:]))
 
@@ -66,7 +75,8 @@ def tile_picked_ohhratio_none_po_kernel(
             dst = grouped[i][half][:].rearrange("p t m j -> p m j t")
             if on_vector > 0:
                 nc.vector.tensor_copy(dst[:, :on_vector], src[:, :on_vector])
-            nc.scalar.copy(dst[:, on_vector:], src[:, on_vector:])
+            if on_vector < P:
+                nc.scalar.copy(dst[:, on_vector:], src[:, on_vector:])
 
         def quantise(i, half, u0=0, u1=2):
             nc.vector.quantize_mx(
@@ -91,10 +101,10 @@ def tile_picked_ohhratio_none_po_kernel(
         deal(0, 0, 0)
         deal(0, 1, 64)
         quantise(0, 0)
-        deal(1, 0, 88)
+        quantise(0, 1)
+        deal(1, 0, 80)
         quantise(1, 0, 0, 1)
         quantise(1, 0, 1, 2)
-        quantise(0, 1)
         deal(1, 1, 32)
         quantise(1, 1)
 
@@ -103,9 +113,9 @@ def tile_picked_ohhratio_none_po_kernel(
         for c in range(2):
             product(first[c], 0, c * W, W, (0, 1))
         for t in range(1, PACK):
-            product(banks[t], t, 0, S, (1, 0))
+            product(banks[t], t, 0, S, (0, 1) if t < 2 else (1, 0))
 
-        h = [keep.tile([P, S], F32, name=f"h{t}") for t in range(PACK)]
+        h = {0: keep.tile([P, S], F32, name="h0", tag="h_a")}
         pa = [keep.tile([P, W], F32, name=f"pa{t}") for t in range(PACK)]
         pb = [keep.tile([P, W], F32, name=f"pb{t}") for t in range(PACK)]
         size = [keep.tile([P, W], F32, name=f"size{t}") for t in range(PACK)]
@@ -116,6 +126,7 @@ def tile_picked_ohhratio_none_po_kernel(
         rows = out_0.rearrange("(p t) c -> p t c", t=PACK)
 
         def fetch_steps(t):
+            h[t] = keep.tile([P, S], F32, name=f"h{t}", tag="h_b" if t == 2 else "h_a")
             return [
                 lambda: nc.scalar.copy(h[t][:], banks[t][:]),
                 lambda: nc.scalar.activation(pb[t][:], h[t][:].indirect(n2_sb[:]), ACT.Copy),
@@ -133,14 +144,19 @@ def tile_picked_ohhratio_none_po_kernel(
         nc.scalar.copy(h[0][:, W:], first[1][:])
         nc.scalar.activation(pb[0][:], h[0][:].indirect(n2_sb[:]), ACT.Copy)
         nc.vector.tensor_copy(pa[0][:], h[0][:].indirect(n1_sb[:]))
-        for t in range(PACK):
-            if t + 1 < PACK:
-                for fetch, inverse in zip(fetch_steps(t + 1), inverse_steps(t)):
-                    fetch()
-                    inverse()
-            else:
-                for inverse in inverse_steps(t):
-                    inverse()
+        absolute, inverse_root, square = zip(*[inverse_steps(t) for t in range(PACK)])
+        empty, fetch_b, fetch_a = fetch_steps(1)
+        for step in (empty, absolute[0], fetch_b, fetch_a):
+            step()
+        empty, fetch_b, fetch_a = fetch_steps(2)
+        for step in (empty, inverse_root[0], fetch_b, fetch_a, square[0]):
+            step()
+        empty, fetch_b, fetch_a = fetch_steps(3)
+        for step in (empty, absolute[1], fetch_b, inverse_root[1], fetch_a, square[1]):
+            step()
+        for steps in (absolute, inverse_root, square):
+            steps[2]()
+            steps[3]()
 
         def put_larger(t):
             nc.vector.tensor_copy(y[t][:].indirect(n2_sb[:]), larger[t][:])
@@ -151,9 +167,10 @@ def tile_picked_ohhratio_none_po_kernel(
 
         for t in range(PACK):
             nc.vector.tensor_tensor(larger[t][:], pa[t][:], pb[t][:], ALU.max)
-            if t > 0:
-                put_ratio(t - 1)
+            if t > 1:
+                put_ratio(t - 2)
             put_larger(t)
+        put_ratio(PACK - 2)
         put_ratio(PACK - 1)
 
         pairs = keep.tile([P, 2, S, 2], BF16, name="pairs", align_bytes=64)

from contextlib import ExitStack

import concourse.mybir as mybir

K, T, S, N, W = 512, 2048, 512, 512, 256
FLOPS = 2 * 2 * K * N * S

F32 = mybir.dt.float32
BF16 = mybir.dt.bfloat16
I32 = mybir.dt.int32
U32 = mybir.dt.uint32
U16 = mybir.dt.uint16
U8 = mybir.dt.uint8
FP8X4 = mybir.dt.float8_e4m3fn_x4
ACT = mybir.ActivationFunctionType
ALU = mybir.AluOpType

P = 128
PACK = 4


def tile_picked_ohhratio_none_po_kernel(
    tc, x_words, x_scales, w1, w2, offs, hz, n1, n2, out_0, out_1, out_2
):
    nc = tc.nc
    with ExitStack() as ctx:
        keep = ctx.enter_context(tc.tile_pool(name="keep", bufs=1))
        psum = ctx.enter_context(tc.psum_pool(name="psum", bufs=1))

        offs_sb = keep.tile([P, S // 16], U16, name="offs_sb")
        hz_sb = keep.tile([P, S // 16], U16, name="hz_sb")
        n1_sb = keep.tile([P, W // 16], U16, name="n1_sb")
        n2_sb = keep.tile([P, W // 16], U16, name="n2_sb")
        scale_table = keep.tile([P, T], U8, name="scale_table", align_bytes=64)
        word_table = keep.tile([P, T], U32, name="word_table", align_bytes=64)
        x_plane = keep.tile([P, 2 * S], U8, name="x_plane", align_bytes=64)
        raw = [keep.tile([P, PACK, N], F32, name=f"raw{i}", align_bytes=64) for i in range(2)]

        nc.vector.memset(scale_table[:].bitcast(I32), 0)
        nc.gpsimd.memset(x_plane[:].bitcast(I32), 0)
        w1_rows = w1.rearrange("(p j) m -> p j m", j=PACK)
        nc.sync.dma_start(raw[0][:, 0:2, :], w1_rows[:, 0:2, :])
        nc.sync.dma_start(offs_sb[:], offs)
        nc.sync.dma_start(hz_sb[:], hz)
        nc.sync.dma_start(scale_table[0:P:8, :].bitcast(I32), x_scales[0].bitcast(I32))
        warm_in = keep.tile([P, 1], F32, name="warm_in")
        warm_out = keep.tile([P, 1], F32, name="warm_out")
        nc.gpsimd.memset(warm_in[:], 1.0)
        nc.scalar.activation(warm_out[:], warm_in[:], ACT.Abs_reciprocal_sqrt, bias=0.5)
        nc.sync.dma_start(word_table[:].bitcast(I32), x_words[0].rearrange("p c r -> p (c r)").bitcast(I32))
        w2_rows = w2.rearrange("(p j) m -> p j m", j=PACK)
        nc.sync.dma_start(raw[0][:, 2:4, :], w1_rows[:, 2:4, :])
        nc.sync.dma_start(raw[1][:, 0:3, :], w2_rows[:, 0:3, :])

        picked_scales = keep.tile([P, 2 * S], U8, name="picked_scales", align_bytes=64)
        picked_words = [keep.tile([P, S], U32, name=f"picked_words{i}", align_bytes=64) for i in range(2)]
        lists = (offs_sb, hz_sb)
        for i in range(2):
            nc.vector.tensor_copy(picked_scales[:, i * S : (i + 1) * S], scale_table[:].indirect(lists[i][:]))
        for i in range(PACK):
            queue = nc.sync if i % 2 == 0 else nc.scalar
            queue.dma_start(x_plane[i:P:32, :].bitcast(I32), picked_scales[8 * i : P : 32, :].bitcast(I32))
        nc.sync.dma_start(raw[1][:, 3:4, :], w2_rows[:, 3:4, :])
        nc.sync.dma_start(n2_sb[:], n2)
        nc.sync.dma_start(n1_sb[:], n1)
        for i in range(2):
            nc.vector.tensor_copy(picked_words[i][:], word_table[:].indirect(lists[i][:]))

        grouped = [[keep.tile([P, 2, P, PACK], BF16, name=f"grouped{i}{half}", align_bytes=64) for half in range(2)] for i in range(2)]
        codes = [[keep.tile([P, 2 * P], U32, name=f"codes{i}{half}", align_bytes=64) for half in range(2)] for i in range(2)]
        scales = [[keep.tile([P, 2 * P], U8, name=f"scales{i}{half}", align_bytes=64) for half in range(2)] for i in range(2)]

        def deal(i, half, on_vector):
            src = raw[i][:].rearrange("p j (m t) -> p m j t", t=PACK)[:, :, :, 2 * half : 2 * half + 2]
            dst = grouped[i][half][:].rearrange("p t m j -> p m j t")
            if on_vector > 0:
                nc.vector.tensor_copy(dst[:, :on_vector], src[:, :on_vector])
            if on_vector < P:
                nc.scalar.copy(dst[:, on_vector:], src[:, on_vector:])

        def quantise(i, half, u0=0, u1=2):
            nc.vector.quantize_mx(
                codes[i][half][:, u0 * P : u1 * P].bitcast(FP8X4),
                scales[i][half][:, u0 * P : u1 * P],
                grouped[i][half][:, u0:u1].rearrange("p t m j -> p (t m j)"),
            )

        def product(bank, t, c0, width, order):
            half, cols = t // 2, slice(t % 2 * P, (t % 2 + 1) * P)
            for i in order:
                nc.tensor.matmul_mx(
                    out=bank[:],
                    lhsT=codes[i][half][:, cols].bitcast(FP8X4),
                    lhsT_scale=scales[i][half][:, cols],
                    rhs=picked_words[i][:, c0 : c0 + width].bitcast(FP8X4),
                    rhs_scale=x_plane[:, i * S + c0 : i * S + c0 + width],
                    start=(i == order[0]),
                    stop=(i == order[1]),
                )

        deal(0, 0, 0)
        deal(0, 1, 64)
        quantise(0, 0)
        quantise(0, 1)
        deal(1, 0, 80)
        quantise(1, 0, 0, 1)
        quantise(1, 0, 1, 2)
        deal(1, 1, 32)
        quantise(1, 1)

        first = [psum.tile([P, W], F32, name=f"first{c}") for c in range(2)]
        banks = {t: psum.tile([P, S], F32, name=f"bank{t}") for t in range(1, PACK)}
        for c in range(2):
            product(first[c], 0, c * W, W, (0, 1))
        for t in range(1, PACK):
            product(banks[t], t, 0, S, (0, 1) if t < 2 else (1, 0))

        h = {0: keep.tile([P, S], F32, name="h0", tag="h_a")}
        pa = [keep.tile([P, W], F32, name=f"pa{t}") for t in range(PACK)]
        pb = [keep.tile([P, W], F32, name=f"pb{t}") for t in range(PACK)]
        size = [keep.tile([P, W], F32, name=f"size{t}") for t in range(PACK)]
        root = [keep.tile([P, W], F32, name=f"root{t}") for t in range(PACK)]
        inv = [keep.tile([P, W], F32, name=f"inv{t}") for t in range(PACK)]
        larger = [keep.tile([P, W], F32, name=f"larger{t}") for t in range(PACK)]
        y = [keep.tile([P, S], F32, name=f"y{t}") for t in range(PACK)]
        rows = out_0.rearrange("(p t) c -> p t c", t=PACK)

        def fetch_steps(t):
            h[t] = keep.tile([P, S], F32, name=f"h{t}", tag="h_b" if t == 2 else "h_a")
            return [
                lambda: nc.scalar.copy(h[t][:], banks[t][:]),
                lambda: nc.scalar.activation(pb[t][:], h[t][:].indirect(n2_sb[:]), ACT.Copy),
                lambda: nc.scalar.activation(pa[t][:], h[t][:].indirect(n1_sb[:]), ACT.Copy),
            ]

        def inverse_steps(t):
            return [
                lambda: nc.scalar.activation(size[t][:], pb[t][:], ACT.Abs),
                lambda: nc.scalar.activation(root[t][:], size[t][:], ACT.Abs_reciprocal_sqrt, bias=0.5),
                lambda: nc.scalar.activation(inv[t][:], root[t][:], ACT.Square),
            ]

        nc.vector.tensor_copy(h[0][:, :W], first[0][:])
        nc.scalar.copy(h[0][:, W:], first[1][:])
        nc.scalar.activation(pb[0][:], h[0][:].indirect(n2_sb[:]), ACT.Copy)
        nc.vector.tensor_copy(pa[0][:], h[0][:].indirect(n1_sb[:]))
        absolute, inverse_root, square = zip(*[inverse_steps(t) for t in range(PACK)])
        empty, fetch_b, fetch_a = fetch_steps(1)
        for step in (empty, absolute[0], fetch_b, fetch_a):
            step()
        empty, fetch_b, fetch_a = fetch_steps(2)
        for step in (empty, inverse_root[0], fetch_b, fetch_a, square[0]):
            step()
        empty, fetch_b, fetch_a = fetch_steps(3)
        for step in (empty, absolute[1], fetch_b, inverse_root[1], fetch_a, square[1]):
            step()
        for steps in (absolute, inverse_root, square):
            steps[2]()
            steps[3]()

        def put_larger(t):
            nc.vector.tensor_copy(y[t][:].indirect(n2_sb[:]), larger[t][:])

        def put_ratio(t):
            nc.vector.tensor_tensor(y[t][:].indirect(n1_sb[:]), pa[t][:], inv[t][:], ALU.mult)
            nc.sync.dma_start(rows[:, t, :], y[t][:])

        for t in range(PACK):
            nc.vector.tensor_tensor(larger[t][:], pa[t][:], pb[t][:], ALU.max)
            if t > 1:
                put_ratio(t - 2)
            put_larger(t)
        put_ratio(PACK - 2)
        put_ratio(PACK - 1)

        pairs = keep.tile([P, 2, S, 2], BF16, name="pairs", align_bytes=64)
        y_grouped = keep.tile([P, S, 2], I32, name="y_grouped", align_bytes=64)
        y_codes = keep.tile([P, S], U32, name="y_codes", align_bytes=64)
        y_scales = keep.tile([P, S], U8, name="y_scales", align_bytes=64)
        word_rows = out_1[0].rearrange("p c r -> p (c r)").bitcast(I32)
        pair_words = pairs[:].rearrange("p u c e -> p u (c e)").bitcast(I32)
        for t in range(PACK - 1):
            nc.scalar.copy(pairs[:, t // 2, :, t % 2], y[t][:])
        halves = [slice(c * W, (c + 1) * W) for c in range(2)]
        for cols in halves:
            nc.scalar.copy(pairs[:, 1, cols, 1], y[PACK - 1][:, cols])
        for cols in halves:
            nc.vector.tensor_copy(y_grouped[:, cols, :], pair_words[:, :, cols].rearrange("p u c -> p c u"))
        for cols in halves:
            nc.vector.quantize_mx(
                y_codes[:, cols].bitcast(FP8X4),
                y_scales[:, cols],
                y_grouped[:, cols, :].rearrange("p c u -> p (c u)").bitcast(BF16),
            )
            nc.sync.dma_start(word_rows[:, cols], y_codes[:, cols].bitcast(I32))
        for q in range(4):
            queue = nc.sync if q == 0 else nc.scalar
            queue.dma_start(out_2[0][4 * q : 4 * q + 4, :].bitcast(I32), y_scales[32 * q : 32 * q + 4, :].bitcast(I32))
